import numpy as np
import ml_dtypes


def mxq(x, axis, fmt="e4m3"):
    dtype, down = {"e4m3": (ml_dtypes.float8_e4m3fn, 7), "e5m2": (ml_dtypes.float8_e5m2, 14)}[fmt]
    v = np.moveaxis(np.asarray(x, np.float32).astype(ml_dtypes.bfloat16).astype(np.float64), axis, -1)
    blocks = v.reshape(v.shape[:-1] + (-1, 32))
    amax = np.abs(blocks).max(-1, keepdims=True)
    byte = np.maximum(np.where(amax > 0, np.frexp(amax)[1] - 1 + 127, 0) - down, 1)
    scale = np.exp2(byte - 127.0)
    codes = (blocks / scale).astype(np.float32).astype(dtype).astype(np.float64)
    return np.moveaxis((codes * scale).reshape(v.shape), -1, axis)


WIDE = False


def mx_kscale(k):
    if not WIDE:
        return np.ones(k)
    levels = np.array([30, -30])
    if k % 512:
        return np.exp2(np.random.permutation(np.resize(levels, k // 32))).repeat(32)
    a = np.empty((k // 512, 16))
    for p in range(k // 512):
        a[p, :8] = np.random.permutation(np.resize(levels, 8))
        for g in range(8):
            far = levels[np.abs(levels - a[p, g]) >= 10]
            a[p, g + 8] = far[np.random.randint(len(far))]
    return np.exp2(a.ravel()).repeat(32)


def f64(x):
    return np.asarray(x).astype(np.float64)


def striped(idx):
    return np.tile(np.asarray(idx).reshape(-1, 16).T, (8, 1)).astype(np.uint16)


def unstriped(offs):
    return offs[:16].T.reshape(-1).astype(np.int64)


E2M1 = np.array([0.0, 0.5, 1.0, 1.5, 2.0, 3.0, 4.0, 6.0, -0.0, -0.5, -1.0, -1.5, -2.0, -3.0, -4.0, -6.0])


def pack_weight(w, fmt):
    k, n = w.shape
    w = f64(np.asarray(w, np.float32).astype(ml_dtypes.bfloat16)).reshape(k // 32, 32, n)
    amax = np.abs(w).max(1)
    if fmt in ("e4m3", "e5m2"):
        byte = np.frexp(amax)[1] - 1 + 127 - (7 if fmt == "e4m3" else 14)
    else:
        mant, ex = np.frexp(amax / 6.0)
        byte = np.where(mant > 0.5, ex, ex - 1) + 127
    byte = np.clip(np.where(amax > 0, byte, 1), 1, 254)
    scaled = (w * np.exp2(127.0 - byte)[:, None, :]).reshape(k, n).astype(np.float32)
    by_word = np.ascontiguousarray(scaled.reshape(k // 512, 128, 4, n).transpose(0, 1, 3, 2))
    if fmt in ("e4m3", "e5m2"):
        words = by_word.astype(ml_dtypes.float8_e4m3fn if fmt == "e4m3" else ml_dtypes.float8_e5m2).view(np.uint8)
    else:
        c = by_word.astype(ml_dtypes.float4_e2m1fn).view(np.uint8) & 0xF
        words = (c[..., 0::2] | (c[..., 1::2] << 4)).reshape(k // 512, 128, 2 * n)
    return np.ascontiguousarray(words), np.ascontiguousarray(byte.astype(np.uint8).reshape(k // 512, 16, n))


def unpack_weight(words, scales, fmt):
    g, _, n = scales.shape
    words = np.ascontiguousarray(words).reshape(g, 128, n, -1)
    if fmt in ("e4m3", "e5m2"):
        vals = words.view(ml_dtypes.float8_e4m3fn if fmt == "e4m3" else ml_dtypes.float8_e5m2).astype(np.float64)
    else:
        nib = np.empty((g, 128, n, 4), np.uint8)
        nib[..., 0::2] = words & 0xF
        nib[..., 1::2] = words >> 4
        vals = E2M1[nib]
    vals = vals * np.repeat(np.exp2(scales.astype(np.float64) - 127.0), 8, axis=1)[..., None]
    return vals.transpose(0, 1, 3, 2).reshape(g * 512, n)


def bf(x):
    return np.asarray(x, np.float32).astype(ml_dtypes.bfloat16)


def planes(Y):
    r, m = Y.shape
    b = f64(bf(Y)).reshape(r // 32, 32, m)
    amax = np.abs(b).max(1)
    byte = np.clip(np.where(amax > 0, np.frexp(amax)[1] - 1 + 127 - 7, 1), 1, 254)
    codes = (b * np.exp2(127.0 - byte)[:, None, :]).reshape(r, m).astype(np.float32).astype(ml_dtypes.float8_e4m3fn).view(np.uint8)
    words = codes.reshape(r // 512, 128, 4, m).transpose(0, 1, 3, 2)
    return np.ascontiguousarray(words), np.ascontiguousarray(byte.astype(np.uint8).reshape(r // 512, 16, m))


K, T, J, S, R, N, Z = 1024, 1024, 384, 512, 512, 512, 512


def setup_inputs():
    n = np.random.standard_normal
    idx = np.random.permutation(T)[:J]
    idx2 = np.random.permutation(S)[:J]
    idx3 = np.random.permutation(Z)[:J]
    fk = mx_kscale(K)
    fr = mx_kscale(R)
    wp = pack_weight(n((K, R)) * 1 / np.sqrt(K) * fk[:, None] * fr, "e5m2")
    wbp = pack_weight(n((R, N)) * 1 / np.sqrt(R) / fr[:, None], "e5m2")
    return {
        "xa": (n((K, T))).astype(np.float32),
        "xb": (n((K, S))).astype(np.float32),
        "hb": (np.random.uniform(0.2, 0.9, (K, 1))).astype(np.float32),
        "fk": (np.random.uniform(0.5, 2.0, (K, 1)) / fk[:, None]).astype(np.float32),
        "w_words": wp[0],
        "w_scales": wp[1],
        "wb_words": wbp[0],
        "wb_scales": wbp[1],
        "tz": (n((N, Z)) * 0.6).astype(np.float32),
        "rw": (np.random.uniform(0.5, 2.0, (1, J))).astype(np.float32),
        "offs": striped(idx),
        "offs2": striped(idx2),
        "offs3": striped(idx3),
    }


def reference(xa, xb, hb, fk, w_words, w_scales, wb_words, wb_scales, tz, rw, offs, offs2, offs3):
    idx = unstriped(offs)
    idx2 = unstriped(offs2)
    idx3 = unstriped(offs3)
    wu = unpack_weight(w_words, w_scales, "e5m2")
    wbu = unpack_weight(wb_words, wb_scales, "e5m2")
    u = (f64(xa)[:, idx] - np.minimum(f64(xb)[:, idx2], f64(hb))) * f64(fk)
    uq = mxq(u, 0, "e4m3")
    a = wu.T @ uq
    pk1 = np.max(a, axis=1, keepdims=True)
    hid = np.maximum(a - 0.4 * pk1, 0.0)
    hidq = mxq(hid, 0, "e4m3")
    p = wbu.T @ hidq
    y = np.maximum(p, f64(tz)[:, idx3]) * f64(rw)
    words, scales = planes(y)
    return y, words, scales

@@ -1,0 +1,251 @@
+from contextlib import ExitStack
+
+import concourse.mybir as mybir
+from concourse.masks import make_identity
+
+K, T, J, S, R, N, Z = 1024, 1024, 384, 512, 512, 512, 512
+FLOPS = 2 * K * R * J + 2 * R * N * J
+
+F32 = mybir.dt.float32
+BF16 = mybir.dt.bfloat16
+I32 = mybir.dt.int32
+U32 = mybir.dt.uint32
+U16 = mybir.dt.uint16
+U8 = mybir.dt.uint8
+E4M3 = mybir.dt.float8_e4m3fn_x4
+E5M2 = mybir.dt.float8_e5m2_x4
+ALU = mybir.AluOpType
+ACT = mybir.ActivationFunctionType
+
+P = 128
+PACK = 4
+K_PASS = P * PACK
+PASSES = K // K_PASS
+CHUNK = 128
+CHUNKS = J // CHUNK
+QUADRANTS = 4
+PEAK_SHARE = 0.4
+
+
+def rows_of_slot(matrix, g, t):
+    return matrix[g * K_PASS : (g + 1) * K_PASS, :].rearrange("(p t) c -> t p c", t=PACK)[t]
+
+
+def weave(copy, woven, slots, cols):
+    copy(
+        woven[:, cols, :].rearrange("p (c i) t -> p c t i", i=4),
+        slots[:, :, cols].rearrange("p t (c i) -> p c t i", i=4),
+    )
+
+
+def deal(copy, dealt, raw):
+    copy(
+        dealt.rearrange("p (g t m) -> p g m t", t=PACK, m=P),
+        raw.rearrange("p (g m t) -> p g m t", t=PACK, m=P),
+    )
+
+
+def tile_list_boundedgaps_peakgated_floored_pl_kernel(
+    tc, xa, xb, hb, fk, w_words, w_scales, wb_words, wb_scales, tz, rw, offs, offs2, offs3, out_0, out_1, out_2
+):
+    nc = tc.nc
+    chunks = [slice(c * CHUNK, (c + 1) * CHUNK) for c in range(CHUNKS)]
+    with ExitStack() as ctx:
+        keep = ctx.enter_context(tc.tile_pool(name="keep", bufs=1))
+        ring = ctx.enter_context(tc.tile_pool(name="ring", bufs=3))
+        psum = ctx.enter_context(tc.psum_pool(name="psum", bufs=1))
+
+        list_a = keep.tile([P, J // 16], U16, name="list_a")
+        list_b = keep.tile([P, J // 16], U16, name="list_b")
+        list_z = keep.tile([P, J // 16], U16, name="list_z")
+        planes = [(g, t) for g in range(PASSES) for t in range(PACK)]
+        xa_sb = {gt: keep.tile([P, T], F32, name="xa_%d_%d" % gt) for gt in planes}
+        xb_sb = {gt: keep.tile([P, S], F32, name="xb_%d_%d" % gt) for gt in planes}
+        tz_sb = [keep.tile([P, Z], F32, name="tz_%d" % t) for t in range(PACK)]
+        hb_sb = keep.tile([P, PASSES, 8], F32, name="hb_sb")
+        fk_sb = keep.tile([P, PASSES, 8], F32, name="fk_sb")
+        rw_col = keep.tile([P, CHUNKS], F32, name="rw_col")
+        w_raw = [keep.tile([P, R], U32, name="w_raw%d" % g) for g in range(PASSES)]
+        wb_raw = keep.tile([P, N], U32, name="wb_raw")
+        ws_raw = keep.tile([P, PASSES * R], U8, name="ws_raw")
+        wbs_raw = keep.tile([P, N], U8, name="wbs_raw")
+        w_codes = [keep.tile([P, R], U32, name="w_codes%d" % g, align_bytes=64) for g in range(PASSES)]
+        wb_codes = keep.tile([P, N], U32, name="wb_codes", align_bytes=64)
+        w_scale = keep.tile([P, PASSES * R], U8, name="w_scale", align_bytes=64)
+        wb_scale = keep.tile([P, N], U8, name="wb_scale", align_bytes=64)
+        identity = keep.tile([P, P], F32, name="identity")
+
+        nc.vector.memset(ws_raw[:].bitcast(I32), 0)
+        nc.vector.memset(wbs_raw[:].bitcast(I32), 0)
+        make_identity(nc, identity[:])
+
+        def load_words(raw, words):
+            nc.sync.dma_start(raw[:].bitcast(I32), words.rearrange("p n t -> p (n t)").bitcast(I32))
+
+        def load_scale_rows(raw, scales, q):
+            passes = scales.shape[0]
+            nc.sync.dma_start(
+                raw[:].bitcast(I32)[32 * q : 32 * q + 4, :].rearrange("r (g c) -> r g c", g=passes),
+                scales[:, 4 * q : 4 * q + 4, :].bitcast(I32).rearrange("g r c -> r g c"),
+            )
+
+        def load_a(g, t):
+            nc.sync.dma_start(xa_sb[g, t][:], rows_of_slot(xa, g, t))
+
+        def load_b(g, t):
+            nc.sync.dma_start(xb_sb[g, t][:], rows_of_slot(xb, g, t))
+
+        order = [(0, 1), (0, 0), (0, 3), (0, 2), (1, 0), (1, 1), (1, 2), (1, 3)]
+        nc.sync.dma_start(list_b[:], offs2)
+        load_b(*order[0])
+        nc.sync.dma_start(list_a[:], offs)
+        nc.sync.dma_start(hb_sb[:, :, 0:PACK], hb.rearrange("(g p t) o -> p g (t o)", g=PASSES, t=PACK))
+        load_a(*order[0])
+        load_b(*order[1])
+        nc.sync.dma_start(fk_sb[:, :, 0:PACK], fk.rearrange("(g p t) o -> p g (t o)", g=PASSES, t=PACK))
+        for i in range(1, len(order) - 1):
+            load_a(*order[i])
+            load_b(*order[i + 1])
+            if i == 1:
+                with nc.allow_non_contiguous_dma(reason="one weight a partition"):
+                    nc.sync.dma_start(rw_col[:], rw.rearrange("o (c p) -> p (o c)", p=P))
+            if 2 <= i < 2 + QUADRANTS:
+                load_scale_rows(ws_raw, w_scales, i - 2)
+        load_words(w_raw[1], w_words[1])
+        load_words(w_raw[0], w_words[0])
+        nc.sync.dma_start(list_z[:], offs3)
+        load_a(*order[-1])
+        for t in range(PACK):
+            nc.sync.dma_start(tz_sb[t][:], rows_of_slot(tz, 0, t))
+            if t == 0:
+                for q in range(QUADRANTS):
+                    load_scale_rows(wbs_raw, wb_scales, q)
+            if t == 1:
+                load_words(wb_raw, wb_words[0])
+
+        u_codes = [keep.tile([P, J], U32, name="u_codes%d" % g, align_bytes=64) for g in range(PASSES)]
+        u_scale = [keep.tile([P, J], U8, name="u_scale%d" % g, align_bytes=64) for g in range(PASSES)]
+        a_banks = [psum.tile([P, J], F32, name="a_bank%d" % t) for t in range(PACK)]
+        nc.vector.tensor_scalar(fk_sb[:, :, 0:PACK:2], fk_sb[:, :, 0:PACK:2], -1.0, None, ALU.mult)
+        for g in range(PASSES):
+            gaps = keep.tile([P, PACK, J], F32, name="gaps%d" % g)
+            u_woven = keep.tile([P, J, PACK], BF16, name="u_woven%d" % g, align_bytes=64)
+            for t in [slot for group, slot in order if group == g]:
+                picked_b = keep.tile([P, J], F32, name="picked_b_%d_%d" % (g, t))
+                nc.scalar.activation(picked_b[:], xb_sb[g, t][:].indirect(list_b[:]), ACT.Copy)
+                other = keep.tile([P, J], F32, name="other_%d_%d" % (g, t))
+                if t % 2 == 0:
+                    nc.scalar.activation(other[:], xa_sb[g, t][:].indirect(list_a[:]), ACT.Copy)
+                    nc.vector.scalar_tensor_tensor(
+                        gaps[:, t, :], picked_b[:], hb_sb[:, g, t : t + 1], other[:], ALU.min, ALU.subtract
+                    )
+                else:
+                    nc.vector.tensor_scalar(other[:], picked_b[:], hb_sb[:, g, t : t + 1], None, ALU.min)
+                    nc.vector.tensor_tensor(
+                        gaps[:, t, :], xa_sb[g, t][:].indirect(list_a[:]), other[:], ALU.subtract
+                    )
+            early = PACK if g == 0 else PACK - 1
+            nc.vector.tensor_tensor(
+                u_woven[:, :, 0:early].rearrange("p (c i) t -> p c t i", i=4),
+                gaps[:, 0:early, :].rearrange("p t (c i) -> p c t i", i=4),
+                fk_sb[:, g, 0:early].unsqueeze(1).unsqueeze(3).to_broadcast([P, J // 4, early, 4]),
+                ALU.mult,
+            )
+            if g == 0:
+                deal(nc.vector.tensor_copy, w_scale[:], ws_raw[:])
+            deal(nc.scalar.copy, w_codes[g][:], w_raw[g][:])
+            halves = [slice(0, 2 * CHUNK), slice(2 * CHUNK, J)]
+            spans = [slice(0, J)] if g == 0 else halves
+            if early < PACK:
+                for cols in spans:
+                    nc.vector.tensor_scalar(
+                        u_woven[:, cols, early], gaps[:, early, cols], fk_sb[:, g, early : early + 1], None, ALU.mult
+                    )
+            for cols in spans:
+                nc.vector.quantize_mx(
+                    out=u_codes[g][:, cols].bitcast(E4M3),
+                    scales=u_scale[g][:, cols],
+                    in_=u_woven[:, cols, :].rearrange("p j t -> p (j t)"),
+                )
+            for t in range(PACK):
+                for cols in halves:
+                    nc.tensor.matmul_mx(
+                        out=a_banks[t][:, cols],
+                        lhsT=w_codes[g][:, t * P : (t + 1) * P].bitcast(E5M2),
+                        lhsT_scale=w_scale[:, g * R + t * P : g * R + (t + 1) * P],
+                        rhs=u_codes[g][:, cols].bitcast(E4M3),
+                        rhs_scale=u_scale[g][:, cols],
+                        start=(g == 0 and cols.start == 0),
+                        stop=(g == PASSES - 1 and cols.stop == J),
+                    )
+
+        deal(nc.vector.tensor_copy, wb_codes[:], wb_raw[:])
+        deal(nc.vector.tensor_copy, wb_scale[:], wbs_raw[:])
+
+        rw_bank = psum.tile([P, J], F32, name="rw_bank")
+        for c in range(CHUNKS):
+            nc.tensor.transpose(rw_bank[:, chunks[c]], rw_col[:, c : c + 1].to_broadcast([P, P]), identity[:])
+
+        floor = keep.tile([P, PACK, J], F32, name="floor")
+        threshold = floor[:, PACK - 1, 0:PACK]
+        hid_slots = keep.tile([P, PACK, J], BF16, name="hid_slots")
+        hid_woven = keep.tile([P, J, PACK], BF16, name="hid_woven", align_bytes=64)
+        hid_codes = keep.tile([P, J], U32, name="hid_codes", align_bytes=64)
+        hid_scale = keep.tile([P, J], U8, name="hid_scale", align_bytes=64)
+        for t in range(PACK):
+            scaled = ring.tile([P, J], F32, name="scaled")
+            nc.vector.tensor_scalar(
+                scaled[:], a_banks[t][:], -PEAK_SHARE, None, ALU.mult, ALU.min, accum_out=threshold[:, t : t + 1]
+            )
+            for cols in chunks if t == PACK - 1 else [slice(0, J)]:
+                nc.scalar.activation(hid_slots[:, t, cols], a_banks[t][:, cols], ACT.Relu, bias=threshold[:, t : t + 1])
+
+        for t in range(PACK):
+            nc.scalar.activation(floor[:, t, :], tz_sb[t][:].indirect(list_z[:]), ACT.Copy)
+
+        p_banks = [psum.tile([P, PACK, CHUNK], F32, name="p_bank%d" % c) for c in range(CHUNKS)]
+        for c, cols in enumerate(chunks):
+            weave(nc.vector.tensor_copy, hid_woven, hid_slots, cols)
+        for c, cols in enumerate(chunks):
+            nc.vector.quantize_mx(
+                out=hid_codes[:, cols].bitcast(E4M3),
+                scales=hid_scale[:, cols],
+                in_=hid_woven[:, cols, :].rearrange("p j t -> p (j t)"),
+            )
+            for t in range(PACK):
+                nc.tensor.matmul_mx(
+                    out=p_banks[c][:, t, :],
+                    lhsT=wb_codes[:, t * P : (t + 1) * P].bitcast(E5M2),
+                    lhsT_scale=wb_scale[:, t * P : (t + 1) * P],
+                    rhs=hid_codes[:, cols].bitcast(E4M3),
+                    rhs_scale=hid_scale[:, cols],
+                    start=True,
+                    stop=True,
+                )
+
+        y_codes = keep.tile([P, J], U32, name="y_codes", align_bytes=64)
+        y_scale = keep.tile([P, J], U8, name="y_scale", align_bytes=64)
+        out_rows = out_0.rearrange("(p t) j -> p t j", t=PACK)
+        out_words = out_1[0].rearrange("p j t -> p (j t)").bitcast(I32)
+        for c, cols in enumerate(chunks):
+            floored = ring.tile([P, PACK, CHUNK], F32, name="floored")
+            y = ring.tile([P, PACK, CHUNK], F32, name="y")
+            y_woven = ring.tile([P, CHUNK, PACK], BF16, name="y_woven", align_bytes=64)
+            nc.vector.tensor_tensor(floored[:], p_banks[c][:], floor[:, :, cols], ALU.max)
+            nc.vector.tensor_tensor(
+                y[:], floored[:], rw_bank[:, cols].unsqueeze(1).to_broadcast([P, PACK, CHUNK]), ALU.mult
+            )
+            nc.sync.dma_start(out_rows[:, :, cols], y[:])
+            copy = nc.vector.tensor_copy if c == CHUNKS - 1 else nc.scalar.copy
+            weave(copy, y_woven, y, slice(0, CHUNK))
+            nc.vector.quantize_mx(
+                out=y_codes[:, cols].bitcast(E4M3),
+                scales=y_scale[:, cols],
+                in_=y_woven[:].rearrange("p j t -> p (j t)"),
+            )
+            nc.sync.dma_start(out_words[:, cols], y_codes[:, cols].bitcast(I32))
+        for q in range(QUADRANTS):
+            queue = nc.sync if q % 2 == 0 else nc.scalar
+            queue.dma_start(
+                out_2[0, 4 * q : 4 * q + 4, :].bitcast(I32), y_scale[:].bitcast(I32)[32 * q : 32 * q + 4, :]
+            )

@@ -31,6 +31,24 @@ def rows_of_slot(matrix, g, t):
     return matrix[g * K_PASS : (g + 1) * K_PASS, :].rearrange("(p t) c -> t p c", t=PACK)[t]
 
 
+def rows_of_slot_pair(matrix, g, h):
+    rows = matrix[g * K_PASS : (g + 1) * K_PASS, :].rearrange("(p h e) c -> h p (e c)", h=2, e=2)
+    return rows[h]
+
+
+def pick_from_pair(nc, picked, pair, e, offsets, entries):
+    width = pair.shape[1] // 2
+    window = pair[:] if e == 0 else pair[:, width:]
+    count = entries.stop - entries.start
+    step = count if 2 * count <= window.shape[1] else count // 2
+    for first in range(entries.start, entries.stop, step):
+        nc.scalar.activation(
+            picked[:, first : first + step],
+            window.indirect(offsets[:, first // 16 : (first + step) // 16]),
+            ACT.Copy,
+        )
+
+
 def weave(copy, woven, slots, cols):
     copy(
         woven[:, cols, :].rearrange("p (c i) t -> p c t i", i=4),
@@ -60,8 +78,9 @@ def tile_list_boundedgaps_peakgated_floored_pl_kernel(
         list_z = keep.tile([P, J // 16], U16, name="list_z")
         planes = [(g, t) for g in range(PASSES) for t in range(PACK)]
         xa_sb = {gt: keep.tile([P, T], F32, name="xa_%d_%d" % gt) for gt in planes}
-        xb_sb = {gt: keep.tile([P, S], F32, name="xb_%d_%d" % gt) for gt in planes}
-        tz_sb = [keep.tile([P, Z], F32, name="tz_%d" % t) for t in range(PACK)]
+        xb_sb = {(g, h): keep.tile([P, 2 * S], F32, name="xb_%d_%d" % (g, h)) for g in range(PASSES) for h in range(2)}
+        tz_low = keep.tile([P, 2 * Z], F32, name="tz_low")
+        gaps = [keep.tile([P, PACK, J], F32, name="gaps%d" % g, tag="gaps%d" % g) for g in range(PASSES)]
         hb_sb = keep.tile([P, PASSES, 8], F32, name="hb_sb")
         fk_sb = keep.tile([P, PASSES, 8], F32, name="fk_sb")
         rw_col = keep.tile([P, CHUNKS], F32, name="rw_col")
@@ -77,7 +96,6 @@ def tile_list_boundedgaps_peakgated_floored_pl_kernel(
 
         nc.vector.memset(ws_raw[:].bitcast(I32), 0)
         nc.vector.memset(wbs_raw[:].bitcast(I32), 0)
-        make_identity(nc, identity[:])
 
         def load_words(raw, words):
             nc.sync.dma_start(raw[:].bitcast(I32), words.rearrange("p n t -> p (n t)").bitcast(I32))
@@ -92,75 +110,79 @@ def tile_list_boundedgaps_peakgated_floored_pl_kernel(
         def load_a(g, t):
             nc.sync.dma_start(xa_sb[g, t][:], rows_of_slot(xa, g, t))
 
-        def load_b(g, t):
-            nc.sync.dma_start(xb_sb[g, t][:], rows_of_slot(xb, g, t))
+        def load_b(g, h):
+            nc.sync.dma_start(xb_sb[g, h][:], rows_of_slot_pair(xb, g, h))
 
-        order = [(0, 1), (0, 0), (0, 3), (0, 2), (1, 0), (1, 1), (1, 2), (1, 3)]
+        make_identity(nc, identity[:])
+
+        nc.scalar.dma_start(hb_sb[:, :, 0:PACK], hb.rearrange("(g p t) o -> p g (t o)", g=PASSES, t=PACK))
+        nc.scalar.dma_start(fk_sb[:, :, 0:PACK], fk.rearrange("(g p t) o -> p g (t o)", g=PASSES, t=PACK))
         nc.sync.dma_start(list_b[:], offs2)
-        load_b(*order[0])
+        load_b(0, 0)
         nc.sync.dma_start(list_a[:], offs)
-        nc.sync.dma_start(hb_sb[:, :, 0:PACK], hb.rearrange("(g p t) o -> p g (t o)", g=PASSES, t=PACK))
-        load_a(*order[0])
-        load_b(*order[1])
-        nc.sync.dma_start(fk_sb[:, :, 0:PACK], fk.rearrange("(g p t) o -> p g (t o)", g=PASSES, t=PACK))
-        for i in range(1, len(order) - 1):
-            load_a(*order[i])
-            load_b(*order[i + 1])
-            if i == 1:
-                with nc.allow_non_contiguous_dma(reason="one weight a partition"):
-                    nc.sync.dma_start(rw_col[:], rw.rearrange("o (c p) -> p (o c)", p=P))
-            if 2 <= i < 2 + QUADRANTS:
-                load_scale_rows(ws_raw, w_scales, i - 2)
-        load_words(w_raw[1], w_words[1])
-        load_words(w_raw[0], w_words[0])
-        nc.sync.dma_start(list_z[:], offs3)
-        load_a(*order[-1])
+        load_a(0, 0)
+        load_b(0, 1)
+        load_a(0, 1)
+        load_scale_rows(ws_raw, w_scales, 0)
+        load_b(1, 0)
+        load_scale_rows(ws_raw, w_scales, 1)
+        load_a(0, 2)
+        load_scale_rows(ws_raw, w_scales, 2)
+        load_a(0, 3)
+        load_scale_rows(ws_raw, w_scales, 3)
+        load_b(1, 1)
         for t in range(PACK):
-            nc.sync.dma_start(tz_sb[t][:], rows_of_slot(tz, 0, t))
-            if t == 0:
-                for q in range(QUADRANTS):
-                    load_scale_rows(wbs_raw, wb_scales, q)
-            if t == 1:
-                load_words(wb_raw, wb_words[0])
+            load_a(1, t)
+        load_words(w_raw[0], w_words[0])
+        load_words(w_raw[1], w_words[1])
+        nc.sync.dma_start(list_z[:], offs3)
+        nc.sync.dma_start(tz_low[:], rows_of_slot_pair(tz, 0, 0))
+        for q in range(QUADRANTS):
+            load_scale_rows(wbs_raw, wb_scales, q)
+        load_words(wb_raw, wb_words[0])
+        with nc.allow_non_contiguous_dma(reason="one weight a partition"):
+            nc.sync.dma_start(rw_col[:], rw.rearrange("o (c p) -> p (o c)", p=P))
 
         u_codes = [keep.tile([P, J], U32, name="u_codes%d" % g, align_bytes=64) for g in range(PASSES)]
         u_scale = [keep.tile([P, J], U8, name="u_scale%d" % g, align_bytes=64) for g in range(PASSES)]
         a_banks = [psum.tile([P, J], F32, name="a_bank%d" % t) for t in range(PACK)]
-        nc.vector.tensor_scalar(fk_sb[:, :, 0:PACK:2], fk_sb[:, :, 0:PACK:2], -1.0, None, ALU.mult)
+        halves = [slice(0, 2 * CHUNK), slice(2 * CHUNK, J)]
+        nc.vector.tensor_scalar(fk_sb[:, 1, 0:3], fk_sb[:, 1, 0:3], -1.0, None, ALU.mult)
         for g in range(PASSES):
-            gaps = keep.tile([P, PACK, J], F32, name="gaps%d" % g)
             u_woven = keep.tile([P, J, PACK], BF16, name="u_woven%d" % g, align_bytes=64)
-            for t in [slot for group, slot in order if group == g]:
+            for t in range(PACK):
                 picked_b = keep.tile([P, J], F32, name="picked_b_%d_%d" % (g, t))
-                nc.scalar.activation(picked_b[:], xb_sb[g, t][:].indirect(list_b[:]), ACT.Copy)
+                pick_from_pair(nc, picked_b, xb_sb[g, t // 2], t % 2, list_b, slice(0, J))
                 other = keep.tile([P, J], F32, name="other_%d_%d" % (g, t))
-                if t % 2 == 0:
+                if g == 1 and t < 3:
                     nc.scalar.activation(other[:], xa_sb[g, t][:].indirect(list_a[:]), ACT.Copy)
                     nc.vector.scalar_tensor_tensor(
-                        gaps[:, t, :], picked_b[:], hb_sb[:, g, t : t + 1], other[:], ALU.min, ALU.subtract
+                        gaps[g][:, t, :], picked_b[:], hb_sb[:, g, t : t + 1], other[:], ALU.min, ALU.subtract
                     )
                 else:
                     nc.vector.tensor_scalar(other[:], picked_b[:], hb_sb[:, g, t : t + 1], None, ALU.min)
+                    fused = J if g == 0 else halves[0].stop
                     nc.vector.tensor_tensor(
-                        gaps[:, t, :], xa_sb[g, t][:].indirect(list_a[:]), other[:], ALU.subtract
+                        gaps[g][:, t, 0:fused],
+                        xa_sb[g, t][:].indirect(list_a[:, 0 : fused // 16]),
+                        other[:, 0:fused],
+                        ALU.subtract,
                     )
-            early = PACK if g == 0 else PACK - 1
-            nc.vector.tensor_tensor(
-                u_woven[:, :, 0:early].rearrange("p (c i) t -> p c t i", i=4),
-                gaps[:, 0:early, :].rearrange("p t (c i) -> p c t i", i=4),
-                fk_sb[:, g, 0:early].unsqueeze(1).unsqueeze(3).to_broadcast([P, J // 4, early, 4]),
-                ALU.mult,
-            )
+                    if fused < J:
+                        rest = keep.tile([P, J - fused], F32, name="rest")
+                        nc.scalar.activation(rest[:], xa_sb[g, t][:].indirect(list_a[:, fused // 16 :]), ACT.Copy)
+                        nc.vector.tensor_tensor(gaps[g][:, t, fused:], rest[:], other[:, fused:], ALU.subtract)
+            spans = [slice(0, J)] if g == 0 else halves
+            for cols in spans:
+                nc.vector.tensor_tensor(
+                    u_woven[:, cols, :].rearrange("p (c i) t -> p c t i", i=4),
+                    gaps[g][:, :, cols].rearrange("p t (c i) -> p c t i", i=4),
+                    fk_sb[:, g, 0:PACK].unsqueeze(1).unsqueeze(3).to_broadcast([P, (cols.stop - cols.start) // 4, PACK, 4]),
+                    ALU.mult,
+                )
             if g == 0:
                 deal(nc.vector.tensor_copy, w_scale[:], ws_raw[:])
             deal(nc.scalar.copy, w_codes[g][:], w_raw[g][:])
-            halves = [slice(0, 2 * CHUNK), slice(2 * CHUNK, J)]
-            spans = [slice(0, J)] if g == 0 else halves
-            if early < PACK:
-                for cols in spans:
-                    nc.vector.tensor_scalar(
-                        u_woven[:, cols, early], gaps[:, early, cols], fk_sb[:, g, early : early + 1], None, ALU.mult
-                    )
             for cols in spans:
                 nc.vector.quantize_mx(
                     out=u_codes[g][:, cols].bitcast(E4M3),
@@ -179,6 +201,8 @@ def tile_list_boundedgaps_peakgated_floored_pl_kernel(
                         stop=(g == PASSES - 1 and cols.stop == J),
                     )
 
+        tz_high = keep.tile([P, 2 * Z], F32, name="tz_high", tag="gaps1")
+        nc.sync.dma_start(tz_high[:], rows_of_slot_pair(tz, 0, 1))
         deal(nc.vector.tensor_copy, wb_codes[:], wb_raw[:])
         deal(nc.vector.tensor_copy, wb_scale[:], wbs_raw[:])
 
@@ -187,7 +211,7 @@ def tile_list_boundedgaps_peakgated_floored_pl_kernel(
             nc.tensor.transpose(rw_bank[:, chunks[c]], rw_col[:, c : c + 1].to_broadcast([P, P]), identity[:])
 
         floor = keep.tile([P, PACK, J], F32, name="floor")
-        threshold = floor[:, PACK - 1, 0:PACK]
+        threshold = keep.tile([P, PACK], F32, name="threshold")
         hid_slots = keep.tile([P, PACK, J], BF16, name="hid_slots")
         hid_woven = keep.tile([P, J, PACK], BF16, name="hid_woven", align_bytes=64)
         hid_codes = keep.tile([P, J], U32, name="hid_codes", align_bytes=64)
@@ -200,13 +224,15 @@ def tile_list_boundedgaps_peakgated_floored_pl_kernel(
             for cols in chunks if t == PACK - 1 else [slice(0, J)]:
                 nc.scalar.activation(hid_slots[:, t, cols], a_banks[t][:, cols], ACT.Relu, bias=threshold[:, t : t + 1])
 
-        for t in range(PACK):
-            nc.scalar.activation(floor[:, t, :], tz_sb[t][:].indirect(list_z[:]), ACT.Copy)
+        for e in range(2):
+            pick_from_pair(nc, floor[:, e, :], tz_low, e, list_z, slice(0, J))
+        for cols in chunks:
+            for e in range(2):
+                pick_from_pair(nc, floor[:, 2 + e, :], tz_high, e, list_z, cols)
 
         p_banks = [psum.tile([P, PACK, CHUNK], F32, name="p_bank%d" % c) for c in range(CHUNKS)]
         for c, cols in enumerate(chunks):
             weave(nc.vector.tensor_copy, hid_woven, hid_slots, cols)
-        for c, cols in enumerate(chunks):
             nc.vector.quantize_mx(
                 out=hid_codes[:, cols].bitcast(E4M3),
                 scales=hid_scale[:, cols],
@@ -227,23 +253,32 @@ def tile_list_boundedgaps_peakgated_floored_pl_kernel(
         y_scale = keep.tile([P, J], U8, name="y_scale", align_bytes=64)
         out_rows = out_0.rearrange("(p t) j -> p t j", t=PACK)
         out_words = out_1[0].rearrange("p j t -> p (j t)").bitcast(I32)
-        for c, cols in enumerate(chunks):
-            floored = ring.tile([P, PACK, CHUNK], F32, name="floored")
-            y = ring.tile([P, PACK, CHUNK], F32, name="y")
-            y_woven = ring.tile([P, CHUNK, PACK], BF16, name="y_woven", align_bytes=64)
-            nc.vector.tensor_tensor(floored[:], p_banks[c][:], floor[:, :, cols], ALU.max)
-            nc.vector.tensor_tensor(
-                y[:], floored[:], rw_bank[:, cols].unsqueeze(1).to_broadcast([P, PACK, CHUNK]), ALU.mult
-            )
-            nc.sync.dma_start(out_rows[:, :, cols], y[:])
+        floored = [keep.tile([P, PACK, CHUNK], F32, name="floored%d" % c) for c in range(CHUNKS)]
+        y = [keep.tile([P, PACK, CHUNK], F32, name="y%d" % c) for c in range(CHUNKS)]
+        y_woven = [keep.tile([P, CHUNK, PACK], BF16, name="y_woven%d" % c, align_bytes=64) for c in range(CHUNKS)]
+
+        def apply_floor(c):
+            nc.vector.tensor_tensor(floored[c][:], p_banks[c][:], floor[:, :, chunks[c]], ALU.max)
+
+        def apply_weight(c):
+            weight = rw_bank[:, chunks[c]].unsqueeze(1).to_broadcast([P, PACK, CHUNK])
+            nc.vector.tensor_tensor(y[c][:], floored[c][:], weight, ALU.mult)
+            nc.sync.dma_start(out_rows[:, :, chunks[c]], y[c][:])
+
+        def hand_on(c):
             copy = nc.vector.tensor_copy if c == CHUNKS - 1 else nc.scalar.copy
-            weave(copy, y_woven, y, slice(0, CHUNK))
+            weave(copy, y_woven[c], y[c], slice(0, CHUNK))
             nc.vector.quantize_mx(
-                out=y_codes[:, cols].bitcast(E4M3),
-                scales=y_scale[:, cols],
-                in_=y_woven[:].rearrange("p j t -> p (j t)"),
+                out=y_codes[:, chunks[c]].bitcast(E4M3),
+                scales=y_scale[:, chunks[c]],
+                in_=y_woven[c][:].rearrange("p j t -> p (j t)"),
             )
-            nc.sync.dma_start(out_words[:, cols], y_codes[:, cols].bitcast(I32))
+            nc.sync.dma_start(out_words[:, chunks[c]], y_codes[:, chunks[c]].bitcast(I32))
+
+        for step in range(CHUNKS + 2):
+            for stage, c in ((apply_floor, step), (apply_weight, step - 1), (hand_on, step - 2)):
+                if 0 <= c < CHUNKS:
+                    stage(c)
         for q in range(QUADRANTS):
             queue = nc.sync if q % 2 == 0 else nc.scalar
             queue.dma_start(

@@ -128,9 +128,9 @@ def tile_list_boundedgaps_peakgated_floored_pl_kernel(
         load_scale_rows(ws_raw, w_scales, 1)
         load_a(0, 2)
         load_scale_rows(ws_raw, w_scales, 2)
-        load_a(0, 3)
-        load_scale_rows(ws_raw, w_scales, 3)
         load_b(1, 1)
+        load_scale_rows(ws_raw, w_scales, 3)
+        load_a(0, 3)
         for t in range(PACK):
             load_a(1, t)
         load_words(w_raw[0], w_words[0])
@@ -210,6 +210,9 @@ def tile_list_boundedgaps_peakgated_floored_pl_kernel(
         for c in range(CHUNKS):
             nc.tensor.transpose(rw_bank[:, chunks[c]], rw_col[:, c : c + 1].to_broadcast([P, P]), identity[:])
 
+        rw_first = keep.tile([P, CHUNK], F32, name="rw_first")
+        nc.scalar.copy(rw_first[:], rw_bank[:, chunks[0]])
+
         floor = keep.tile([P, PACK, J], F32, name="floor")
         threshold = keep.tile([P, PACK], F32, name="threshold")
         hid_slots = keep.tile([P, PACK, J], BF16, name="hid_slots")
@@ -261,8 +264,10 @@ def tile_list_boundedgaps_peakgated_floored_pl_kernel(
             nc.vector.tensor_tensor(floored[c][:], p_banks[c][:], floor[:, :, chunks[c]], ALU.max)
 
         def apply_weight(c):
-            weight = rw_bank[:, chunks[c]].unsqueeze(1).to_broadcast([P, PACK, CHUNK])
-            nc.vector.tensor_tensor(y[c][:], floored[c][:], weight, ALU.mult)
+            source = rw_first[:] if c == 0 else rw_bank[:, chunks[c]]
+            weight = source.unsqueeze(1).to_broadcast([P, PACK, CHUNK])
+            engine = nc.gpsimd if c == 0 else nc.vector
+            engine.tensor_tensor(y[c][:], floored[c][:], weight, ALU.mult)
             nc.sync.dma_start(out_rows[:, :, chunks[c]], y[c][:])
 
         def hand_on(c):
@@ -273,7 +278,8 @@ def tile_list_boundedgaps_peakgated_floored_pl_kernel(
                 scales=y_scale[:, chunks[c]],
                 in_=y_woven[c][:].rearrange("p j t -> p (j t)"),
             )
-            nc.sync.dma_start(out_words[:, chunks[c]], y_codes[:, chunks[c]].bitcast(I32))
+            queue = nc.scalar if c == CHUNKS - 1 else nc.sync
+            queue.dma_start(out_words[:, chunks[c]], y_codes[:, chunks[c]].bitcast(I32))
 
         for step in range(CHUNKS + 2):
             for stage, c in ((apply_floor, step), (apply_weight, step - 1), (hand_on, step - 2)):

from contextlib import ExitStack

import concourse.mybir as mybir
from concourse.masks import make_identity

K, T, J, S, R, N, Z = 1024, 1024, 384, 512, 512, 512, 512
FLOPS = 2 * K * R * J + 2 * R * N * J

F32 = mybir.dt.float32
BF16 = mybir.dt.bfloat16
I32 = mybir.dt.int32
U32 = mybir.dt.uint32
U16 = mybir.dt.uint16
U8 = mybir.dt.uint8
E4M3 = mybir.dt.float8_e4m3fn_x4
E5M2 = mybir.dt.float8_e5m2_x4
ALU = mybir.AluOpType
ACT = mybir.ActivationFunctionType

P = 128
PACK = 4
K_PASS = P * PACK
PASSES = K // K_PASS
CHUNK = 128
CHUNKS = J // CHUNK
QUADRANTS = 4
PEAK_SHARE = 0.4


def rows_of_slot(matrix, g, t):
    return matrix[g * K_PASS : (g + 1) * K_PASS, :].rearrange("(p t) c -> t p c", t=PACK)[t]


def rows_of_slot_pair(matrix, g, h):
    rows = matrix[g * K_PASS : (g + 1) * K_PASS, :].rearrange("(p h e) c -> h p (e c)", h=2, e=2)
    return rows[h]


def pick_from_pair(nc, picked, pair, e, offsets, entries):
    width = pair.shape[1] // 2
    window = pair[:] if e == 0 else pair[:, width:]
    count = entries.stop - entries.start
    step = count if 2 * count <= window.shape[1] else count // 2
    for first in range(entries.start, entries.stop, step):
        nc.scalar.activation(
            picked[:, first : first + step],
            window.indirect(offsets[:, first // 16 : (first + step) // 16]),
            ACT.Copy,
        )


def weave(copy, woven, slots, cols):
    copy(
        woven[:, cols, :].rearrange("p (c i) t -> p c t i", i=4),
        slots[:, :, cols].rearrange("p t (c i) -> p c t i", i=4),
    )


def deal(copy, dealt, raw):
    copy(
        dealt.rearrange("p (g t m) -> p g m t", t=PACK, m=P),
        raw.rearrange("p (g m t) -> p g m t", t=PACK, m=P),
    )


def tile_list_boundedgaps_peakgated_floored_pl_kernel(
    tc, xa, xb, hb, fk, w_words, w_scales, wb_words, wb_scales, tz, rw, offs, offs2, offs3, out_0, out_1, out_2
):
    nc = tc.nc
    chunks = [slice(c * CHUNK, (c + 1) * CHUNK) for c in range(CHUNKS)]
    with ExitStack() as ctx:
        keep = ctx.enter_context(tc.tile_pool(name="keep", bufs=1))
        ring = ctx.enter_context(tc.tile_pool(name="ring", bufs=3))
        psum = ctx.enter_context(tc.psum_pool(name="psum", bufs=1))

        list_a = keep.tile([P, J // 16], U16, name="list_a")
        list_b = keep.tile([P, J // 16], U16, name="list_b")
        list_z = keep.tile([P, J // 16], U16, name="list_z")
        planes = [(g, t) for g in range(PASSES) for t in range(PACK)]
        xa_sb = {gt: keep.tile([P, T], F32, name="xa_%d_%d" % gt) for gt in planes}
        xb_sb = {(g, h): keep.tile([P, 2 * S], F32, name="xb_%d_%d" % (g, h)) for g in range(PASSES) for h in range(2)}
        tz_low = keep.tile([P, 2 * Z], F32, name="tz_low")
        gaps = [keep.tile([P, PACK, J], F32, name="gaps%d" % g, tag="gaps%d" % g) for g in range(PASSES)]
        hb_sb = keep.tile([P, PASSES, 8], F32, name="hb_sb")
        fk_sb = keep.tile([P, PASSES, 8], F32, name="fk_sb")
        rw_col = keep.tile([P, CHUNKS], F32, name="rw_col")
        w_raw = [keep.tile([P, R], U32, name="w_raw%d" % g) for g in range(PASSES)]
        wb_raw = keep.tile([P, N], U32, name="wb_raw")
        ws_raw = keep.tile([P, PASSES * R], U8, name="ws_raw")
        wbs_raw = keep.tile([P, N], U8, name="wbs_raw")
        w_codes = [keep.tile([P, R], U32, name="w_codes%d" % g, align_bytes=64) for g in range(PASSES)]
        wb_codes = keep.tile([P, N], U32, name="wb_codes", align_bytes=64)
        w_scale = keep.tile([P, PASSES * R], U8, name="w_scale", align_bytes=64)
        wb_scale = keep.tile([P, N], U8, name="wb_scale", align_bytes=64)
        identity = keep.tile([P, P], F32, name="identity")

        nc.vector.memset(ws_raw[:].bitcast(I32), 0)
        nc.vector.memset(wbs_raw[:].bitcast(I32), 0)

        def load_words(raw, words):
            nc.sync.dma_start(raw[:].bitcast(I32), words.rearrange("p n t -> p (n t)").bitcast(I32))

        def load_scale_rows(raw, scales, q):
            passes = scales.shape[0]
            nc.sync.dma_start(
                raw[:].bitcast(I32)[32 * q : 32 * q + 4, :].rearrange("r (g c) -> r g c", g=passes),
                scales[:, 4 * q : 4 * q + 4, :].bitcast(I32).rearrange("g r c -> r g c"),
            )

        def load_a(g, t):
            nc.sync.dma_start(xa_sb[g, t][:], rows_of_slot(xa, g, t))

        def load_b(g, h):
            nc.sync.dma_start(xb_sb[g, h][:], rows_of_slot_pair(xb, g, h))

        make_identity(nc, identity[:])

        nc.scalar.dma_start(hb_sb[:, :, 0:PACK], hb.rearrange("(g p t) o -> p g (t o)", g=PASSES, t=PACK))
        nc.scalar.dma_start(fk_sb[:, :, 0:PACK], fk.rearrange("(g p t) o -> p g (t o)", g=PASSES, t=PACK))
        nc.sync.dma_start(list_b[:], offs2)
        load_b(0, 0)
        nc.sync.dma_start(list_a[:], offs)
        load_a(0, 0)
        load_b(0, 1)
        load_a(0, 1)
        load_scale_rows(ws_raw, w_scales, 0)
        load_b(1, 0)
        load_scale_rows(ws_raw, w_scales, 1)
        load_a(0, 2)
        load_scale_rows(ws_raw, w_scales, 2)
        load_b(1, 1)
        load_scale_rows(ws_raw, w_scales, 3)
        load_a(0, 3)
        for t in range(PACK):
            load_a(1, t)
        load_words(w_raw[0], w_words[0])
        load_words(w_raw[1], w_words[1])
        nc.sync.dma_start(list_z[:], offs3)
        nc.sync.dma_start(tz_low[:], rows_of_slot_pair(tz, 0, 0))
        for q in range(QUADRANTS):
            load_scale_rows(wbs_raw, wb_scales, q)
        load_words(wb_raw, wb_words[0])
        with nc.allow_non_contiguous_dma(reason="one weight a partition"):
            nc.sync.dma_start(rw_col[:], rw.rearrange("o (c p) -> p (o c)", p=P))

        u_codes = [keep.tile([P, J], U32, name="u_codes%d" % g, align_bytes=64) for g in range(PASSES)]
        u_scale = [keep.tile([P, J], U8, name="u_scale%d" % g, align_bytes=64) for g in range(PASSES)]
        a_banks = [psum.tile([P, J], F32, name="a_bank%d" % t) for t in range(PACK)]
        halves = [slice(0, 2 * CHUNK), slice(2 * CHUNK, J)]
        nc.vector.tensor_scalar(fk_sb[:, 1, 0:3], fk_sb[:, 1, 0:3], -1.0, None, ALU.mult)
        for g in range(PASSES):
            u_woven = keep.tile([P, J, PACK], BF16, name="u_woven%d" % g, align_bytes=64)
            for t in range(PACK):
                picked_b = keep.tile([P, J], F32, name="picked_b_%d_%d" % (g, t))
                pick_from_pair(nc, picked_b, xb_sb[g, t // 2], t % 2, list_b, slice(0, J))
                other = keep.tile([P, J], F32, name="other_%d_%d" % (g, t))
                if g == 1 and t < 3:
                    nc.scalar.activation(other[:], xa_sb[g, t][:].indirect(list_a[:]), ACT.Copy)
                    nc.vector.scalar_tensor_tensor(
                        gaps[g][:, t, :], picked_b[:], hb_sb[:, g, t : t + 1], other[:], ALU.min, ALU.subtract
                    )
                else:
                    nc.vector.tensor_scalar(other[:], picked_b[:], hb_sb[:, g, t : t + 1], None, ALU.min)
                    fused = J if g == 0 else halves[0].stop
                    nc.vector.tensor_tensor(
                        gaps[g][:, t, 0:fused],
                        xa_sb[g, t][:].indirect(list_a[:, 0 : fused // 16]),
                        other[:, 0:fused],
                        ALU.subtract,
                    )
                    if fused < J:
                        rest = keep.tile([P, J - fused], F32, name="rest")
                        nc.scalar.activation(rest[:], xa_sb[g, t][:].indirect(list_a[:, fused // 16 :]), ACT.Copy)
                        nc.vector.tensor_tensor(gaps[g][:, t, fused:], rest[:], other[:, fused:], ALU.subtract)
            spans = [slice(0, J)] if g == 0 else halves
            for cols in spans:
                nc.vector.tensor_tensor(
                    u_woven[:, cols, :].rearrange("p (c i) t -> p c t i", i=4),
                    gaps[g][:, :, cols].rearrange("p t (c i) -> p c t i", i=4),
                    fk_sb[:, g, 0:PACK].unsqueeze(1).unsqueeze(3).to_broadcast([P, (cols.stop - cols.start) // 4, PACK, 4]),
                    ALU.mult,
                )
            if g == 0:
                deal(nc.vector.tensor_copy, w_scale[:], ws_raw[:])
            deal(nc.scalar.copy, w_codes[g][:], w_raw[g][:])
            for cols in spans:
                nc.vector.quantize_mx(
                    out=u_codes[g][:, cols].bitcast(E4M3),
                    scales=u_scale[g][:, cols],
                    in_=u_woven[:, cols, :].rearrange("p j t -> p (j t)"),
                )
            for t in range(PACK):
                for cols in halves:
                    nc.tensor.matmul_mx(
                        out=a_banks[t][:, cols],
                        lhsT=w_codes[g][:, t * P : (t + 1) * P].bitcast(E5M2),
                        lhsT_scale=w_scale[:, g * R + t * P : g * R + (t + 1) * P],
                        rhs=u_codes[g][:, cols].bitcast(E4M3),
                        rhs_scale=u_scale[g][:, cols],
                        start=(g == 0 and cols.start == 0),
                        stop=(g == PASSES - 1 and cols.stop == J),
                    )

        tz_high = keep.tile([P, 2 * Z], F32, name="tz_high", tag="gaps1")
        nc.sync.dma_start(tz_high[:], rows_of_slot_pair(tz, 0, 1))
        deal(nc.vector.tensor_copy, wb_codes[:], wb_raw[:])
        deal(nc.vector.tensor_copy, wb_scale[:], wbs_raw[:])

        rw_bank = psum.tile([P, J], F32, name="rw_bank")
        for c in range(CHUNKS):
            nc.tensor.transpose(rw_bank[:, chunks[c]], rw_col[:, c : c + 1].to_broadcast([P, P]), identity[:])

        rw_first = keep.tile([P, CHUNK], F32, name="rw_first")
        nc.scalar.copy(rw_first[:], rw_bank[:, chunks[0]])

        floor = keep.tile([P, PACK, J], F32, name="floor")
        threshold = keep.tile([P, PACK], F32, name="threshold")
        hid_slots = keep.tile([P, PACK, J], BF16, name="hid_slots")
        hid_woven = keep.tile([P, J, PACK], BF16, name="hid_woven", align_bytes=64)
        hid_codes = keep.tile([P, J], U32, name="hid_codes", align_bytes=64)
        hid_scale = keep.tile([P, J], U8, name="hid_scale", align_bytes=64)
        for t in range(PACK):
            scaled = ring.tile([P, J], F32, name="scaled")
            nc.vector.tensor_scalar(
                scaled[:], a_banks[t][:], -PEAK_SHARE, None, ALU.mult, ALU.min, accum_out=threshold[:, t : t + 1]
            )
            for cols in chunks if t == PACK - 1 else [slice(0, J)]:
                nc.scalar.activation(hid_slots[:, t, cols], a_banks[t][:, cols], ACT.Relu, bias=threshold[:, t : t + 1])

        for e in range(2):
            pick_from_pair(nc, floor[:, e, :], tz_low, e, list_z, slice(0, J))
        for cols in chunks:
            for e in range(2):
                pick_from_pair(nc, floor[:, 2 + e, :], tz_high, e, list_z, cols)

        p_banks = [psum.tile([P, PACK, CHUNK], F32, name="p_bank%d" % c) for c in range(CHUNKS)]
        for c, cols in enumerate(chunks):
            weave(nc.vector.tensor_copy, hid_woven, hid_slots, cols)
            nc.vector.quantize_mx(
                out=hid_codes[:, cols].bitcast(E4M3),
                scales=hid_scale[:, cols],
                in_=hid_woven[:, cols, :].rearrange("p j t -> p (j t)"),
            )
            for t in range(PACK):
                nc.tensor.matmul_mx(
                    out=p_banks[c][:, t, :],
                    lhsT=wb_codes[:, t * P : (t + 1) * P].bitcast(E5M2),
                    lhsT_scale=wb_scale[:, t * P : (t + 1) * P],
                    rhs=hid_codes[:, cols].bitcast(E4M3),
                    rhs_scale=hid_scale[:, cols],
                    start=True,
                    stop=True,
                )

        y_codes = keep.tile([P, J], U32, name="y_codes", align_bytes=64)
        y_scale = keep.tile([P, J], U8, name="y_scale", align_bytes=64)
        out_rows = out_0.rearrange("(p t) j -> p t j", t=PACK)
        out_words = out_1[0].rearrange("p j t -> p (j t)").bitcast(I32)
        floored = [keep.tile([P, PACK, CHUNK], F32, name="floored%d" % c) for c in range(CHUNKS)]
        y = [keep.tile([P, PACK, CHUNK], F32, name="y%d" % c) for c in range(CHUNKS)]
        y_woven = [keep.tile([P, CHUNK, PACK], BF16, name="y_woven%d" % c, align_bytes=64) for c in range(CHUNKS)]

        def apply_floor(c):
            nc.vector.tensor_tensor(floored[c][:], p_banks[c][:], floor[:, :, chunks[c]], ALU.max)

        def apply_weight(c):
            source = rw_first[:] if c == 0 else rw_bank[:, chunks[c]]
            weight = source.unsqueeze(1).to_broadcast([P, PACK, CHUNK])
            engine = nc.gpsimd if c == 0 else nc.vector
            engine.tensor_tensor(y[c][:], floored[c][:], weight, ALU.mult)
            nc.sync.dma_start(out_rows[:, :, chunks[c]], y[c][:])

        def hand_on(c):
            copy = nc.vector.tensor_copy if c == CHUNKS - 1 else nc.scalar.copy
            weave(copy, y_woven[c], y[c], slice(0, CHUNK))
            nc.vector.quantize_mx(
                out=y_codes[:, chunks[c]].bitcast(E4M3),
                scales=y_scale[:, chunks[c]],
                in_=y_woven[c][:].rearrange("p j t -> p (j t)"),
            )
            queue = nc.scalar if c == CHUNKS - 1 else nc.sync
            queue.dma_start(out_words[:, chunks[c]], y_codes[:, chunks[c]].bitcast(I32))

        for step in range(CHUNKS + 2):
            for stage, c in ((apply_floor, step), (apply_weight, step - 1), (hand_on, step - 2)):
                if 0 <= c < CHUNKS:
                    stage(c)
        for q in range(QUADRANTS):
            queue = nc.sync if q % 2 == 0 else nc.scalar
            queue.dma_start(
                out_2[0, 4 * q : 4 * q + 4, :].bitcast(I32), y_scale[:].bitcast(I32)[32 * q : 32 * q + 4, :]
            )
